import numpy as np
CORES = [7,15,23,31,39,47,55,63,71,79]
N = 10
T, K = 512, 2
ROUTE = [[[1,5],[2,1],[9,7],[7,3],[2,6],[9,5],[0,3],[0,5],[1,7],[4,0],[3,8],[2,9],[7,1],[6,1],[2,5],[6,4],[2,3],[5,6],[2,8],[7,0],[1,9],[0,1],[7,6],[1,9],[7,0],[1,4],[1,9],[8,5],[8,6],[6,3],[2,5],[8,0],[5,7],[0,7],[0,7],[7,1],[7,3],[3,8],[6,4],[0,9],[8,2],[1,6],[0,4],[7,1],[1,8],[4,8],[4,3],[7,1],[5,6],[5,0],[3,8],[8,3],[5,7],[4,0],[1,0],[4,7],[9,2],[1,6],[7,1],[6,4],[0,7],[1,2],[8,5],[2,4],[8,3],[2,1],[3,2],[3,2],[7,6],[7,0],[5,7],[2,1],[6,0],[1,0],[4,7],[3,7],[2,0],[8,9],[0,7],[1,2],[7,2],[2,3],[8,5],[8,7],[6,0],[4,6],[7,9],[3,0],[4,3],[0,1],[1,3],[2,9],[4,7],[5,4],[3,1],[1,8],[4,1],[5,4],[4,3],[9,4],[3,6],[2,7],[0,1],[9,6],[6,8],[4,0],[5,2],[9,1],[4,9],[7,4],[8,5],[3,4],[1,7],[4,5],[1,7],[8,3],[6,4],[1,6],[4,5],[8,1],[5,0],[1,6],[2,8],[3,9],[9,0],[1,7],[6,8],[8,1],[2,4],[9,4],[9,1],[7,3],[9,5],[1,4],[5,8],[2,7],[4,8],[8,4],[4,7],[5,4],[9,8],[6,4],[5,9],[3,0],[0,4],[4,3],[4,8],[8,9],[4,9],[2,5],[6,8],[4,6],[2,7],[4,8],[5,8],[8,4],[8,0],[1,8],[0,9],[2,5],[6,3],[0,7],[7,8],[6,2],[5,4],[4,6],[6,1],[0,8],[2,5],[9,7],[8,7],[6,5],[6,4],[3,4],[0,8],[8,3],[9,8],[6,3],[0,4],[2,8],[8,3],[1,6],[1,7],[2,6],[7,5],[1,2],[6,5],[5,4],[0,4],[9,0],[7,6],[4,5],[1,5],[7,6],[9,5],[1,9],[7,8],[9,0],[3,9],[6,9],[0,1],[1,6],[0,4],[1,7],[0,2],[8,9],[2,6],[5,0],[5,7],[7,9],[3,2],[9,6],[4,7],[9,4],[1,5],[0,8],[1,3],[5,1],[5,8],[7,9],[1,9],[7,2],[9,2],[8,9],[4,6],[7,3],[2,8],[7,5],[2,9],[9,1],[8,0],[4,8],[4,1],[3,0],[5,4],[1,4],[8,0],[3,0],[0,4],[4,3],[3,7],[3,5],[9,3],[5,9],[2,9],[3,8],[4,1],[5,4],[0,6],[3,2],[2,5],[6,0],[2,9],[3,2],[2,5],[6,5],[7,6],[2,7],[7,4],[3,2],[0,7],[2,1],[1,2],[8,6],[9,5],[5,4],[5,2],[5,8],[7,3],[7,9],[0,4],[8,6],[1,9],[8,4],[9,0],[9,6],[8,0],[7,4],[2,6],[4,6],[0,1],[4,9],[8,2],[1,8],[5,8],[1,3],[2,9],[0,6],[0,2],[9,4],[5,3],[3,0],[7,3],[8,5],[3,2],[8,6],[4,7],[8,0],[6,0],[0,9],[1,2],[8,2],[2,6],[2,9],[5,4],[7,4],[0,2],[9,6],[6,0],[2,5],[7,4],[1,5],[1,4],[1,4],[3,1],[5,4],[6,3],[9,1],[8,6],[9,5],[4,1],[0,2],[8,5],[4,7],[6,0],[5,9],[3,4],[8,6],[4,9],[3,4],[5,4],[1,7],[0,5],[8,7],[5,0],[1,9],[0,7],[3,2],[8,4],[2,9],[5,8],[0,5],[4,6],[5,9],[5,3],[2,5],[8,6],[2,9],[3,4],[7,4],[2,0],[3,0],[2,3],[9,7],[7,6],[6,4],[7,1],[9,8],[6,3],[8,6],[8,7],[4,1],[7,0],[3,5],[7,4],[2,9],[4,0],[0,7],[0,6],[8,4],[8,1],[2,3],[5,8],[1,9],[2,7],[5,3],[4,3],[9,2],[6,9],[2,9],[2,4],[3,6],[5,1],[5,9],[8,6],[1,5],[1,7],[9,1],[9,7],[3,5],[5,8],[2,0],[6,7],[3,8],[8,0],[7,3],[6,9],[8,4],[4,2],[3,7],[8,9],[2,9],[6,3],[2,6],[1,3],[9,5],[0,6],[6,7],[5,1],[4,8],[5,8],[2,3],[4,9],[0,8],[7,3],[7,0],[1,0],[6,2],[6,3],[4,0],[7,5],[4,7],[8,9],[5,3],[2,4],[7,1],[8,5],[3,1],[7,1],[9,2],[4,6],[8,3],[8,6],[9,0],[3,7],[2,9],[8,9],[7,3],[2,1],[3,8],[7,4],[0,2],[6,9],[7,3],[3,0],[4,2],[8,9],[0,3],[6,9],[1,9],[9,8],[6,8],[6,2],[5,6],[2,8],[3,6],[2,0],[5,1],[3,4],[3,8],[2,6],[7,5],[1,0],[5,0],[3,4],[4,9],[8,2],[4,0],[7,3],[9,4],[7,2],[1,0],[7,2],[4,9],[8,4],[2,7],[3,9],[8,3],[4,5],[6,7],[0,2],[5,0],[9,2],[1,0],[7,6],[8,9],[4,9],[9,7],[5,8],[1,4],[5,2],[3,4],[2,4],[4,6],[1,8],[0,6],[8,5],[6,8],[0,1],[4,9],[1,4],[2,3],[1,6],[0,4],[1,9],[8,0],[5,7],[1,2],[1,7],[1,7],[7,2],[0,7]],[[6,2],[3,0],[1,4],[5,0],[4,3],[4,9],[0,8],[4,7],[0,8],[5,0],[7,6],[1,7],[2,3],[0,1],[9,1],[3,5],[5,0],[8,3],[7,0],[0,9],[2,9],[4,3],[8,9],[2,4],[4,8],[4,6],[0,2],[2,8],[8,0],[2,1],[7,4],[2,0],[9,0],[3,5],[6,9],[5,9],[5,7],[7,6],[0,4],[3,1],[3,4],[7,1],[4,3],[2,8],[0,2],[3,7],[4,1],[4,1],[1,9],[0,1],[3,9],[6,0],[8,4],[6,9],[4,7],[7,3],[9,8],[4,1],[4,7],[7,1],[0,6],[3,9],[9,4],[2,9],[9,7],[2,3],[4,0],[5,6],[7,1],[9,0],[4,3],[3,9],[8,7],[7,5],[6,8],[2,0],[5,4],[8,4],[2,1],[3,8],[5,0],[7,6],[4,0],[4,7],[5,7],[5,7],[6,7],[8,3],[7,5],[7,8],[8,2],[7,3],[1,8],[0,1],[1,7],[0,3],[8,2],[6,4],[0,2],[1,8],[5,4],[8,9],[0,4],[5,9],[0,7],[5,2],[1,6],[8,4],[1,3],[8,0],[0,6],[1,4],[1,9],[1,2],[9,8],[7,3],[9,3],[9,8],[1,3],[1,3],[4,5],[7,4],[5,2],[1,3],[7,0],[2,9],[9,0],[7,8],[5,1],[5,1],[9,5],[0,9],[1,3],[8,1],[3,6],[7,9],[2,3],[9,6],[2,8],[1,0],[7,1],[0,3],[9,7],[3,5],[2,8],[7,1],[9,5],[5,2],[2,6],[5,6],[9,1],[8,7],[3,8],[1,6],[3,5],[5,8],[8,1],[1,2],[7,5],[6,9],[3,4],[9,6],[9,3],[3,6],[7,2],[4,5],[9,8],[6,9],[5,9],[6,8],[1,8],[3,0],[9,6],[9,7],[3,9],[8,7],[4,7],[8,7],[7,8],[0,9],[8,1],[6,7],[8,3],[3,8],[2,6],[4,3],[7,0],[7,8],[8,6],[9,3],[2,0],[9,1],[1,0],[8,3],[4,6],[4,5],[8,4],[2,7],[6,1],[2,1],[4,0],[1,6],[6,1],[3,0],[5,0],[7,1],[2,1],[6,7],[9,5],[2,4],[1,2],[5,6],[2,3],[5,3],[0,8],[0,3],[8,7],[7,2],[5,7],[2,6],[2,5],[8,2],[9,0],[1,4],[7,8],[3,2],[4,0],[5,4],[3,8],[3,5],[6,3],[3,5],[5,6],[2,7],[9,0],[1,0],[1,9],[0,7],[7,5],[0,7],[5,8],[1,8],[3,4],[6,5],[5,9],[5,3],[5,7],[8,3],[7,6],[6,9],[0,3],[5,3],[8,3],[4,8],[2,7],[4,3],[4,5],[3,8],[4,1],[0,8],[8,1],[3,5],[2,4],[6,3],[6,1],[0,1],[1,7],[2,7],[3,1],[3,7],[4,6],[1,5],[1,2],[2,6],[7,3],[4,5],[3,4],[0,1],[0,5],[2,6],[1,2],[7,2],[9,5],[1,6],[2,1],[3,2],[6,9],[8,2],[3,8],[9,3],[3,8],[4,9],[7,0],[6,4],[3,0],[1,4],[4,6],[2,8],[3,7],[4,8],[7,1],[2,6],[5,4],[1,5],[1,7],[1,6],[1,7],[6,5],[1,2],[7,9],[9,7],[0,1],[4,6],[7,4],[3,6],[3,0],[9,3],[7,2],[9,5],[5,1],[4,6],[5,1],[3,7],[0,9],[4,7],[7,5],[4,1],[5,9],[1,6],[8,9],[3,1],[3,2],[8,7],[0,3],[0,7],[3,6],[6,0],[2,6],[6,2],[1,7],[2,0],[7,1],[7,8],[1,8],[5,7],[5,2],[5,9],[7,5],[5,7],[5,2],[4,9],[1,7],[6,0],[3,5],[8,3],[9,3],[9,2],[3,9],[2,9],[0,3],[2,6],[0,9],[1,9],[5,7],[8,4],[7,1],[1,9],[5,1],[0,5],[0,5],[6,0],[4,5],[8,1],[4,1],[6,0],[5,2],[7,2],[8,4],[4,5],[8,6],[3,1],[9,5],[2,5],[9,1],[2,3],[5,1],[9,1],[9,2],[3,2],[3,9],[5,7],[8,3],[1,9],[2,0],[6,2],[5,2],[6,3],[5,7],[2,1],[7,3],[7,0],[4,8],[4,9],[7,2],[6,9],[0,7],[6,7],[8,6],[7,6],[9,0],[1,9],[0,6],[5,2],[8,4],[6,3],[1,3],[6,1],[9,0],[8,4],[9,7],[2,4],[1,5],[4,9],[4,8],[9,7],[4,8],[5,1],[1,7],[6,7],[6,5],[1,0],[0,6],[7,8],[3,5],[5,4],[2,0],[5,3],[0,6],[7,6],[6,7],[5,2],[5,9],[3,0],[5,9],[1,5],[1,3],[3,0],[3,9],[7,9],[1,2],[3,6],[4,0],[2,7],[3,2],[4,9],[8,5],[4,5],[8,0],[9,4],[6,3],[6,4],[4,8],[6,4],[1,7],[6,4],[6,9],[3,8],[5,0],[6,5],[6,2],[6,2],[1,5],[1,8],[7,4],[7,3],[1,7],[5,3],[8,7],[4,7],[9,7],[6,3],[6,3],[5,3],[3,0],[5,9],[9,4],[2,5],[4,6],[4,1],[1,8],[2,1],[4,6],[3,8],[9,3],[9,2],[2,7],[8,3],[9,5],[3,7],[5,4],[1,0],[7,2],[8,1],[3,5],[4,2],[5,1],[5,7],[7,8],[2,7],[4,5],[9,5],[7,8]],[[7,0],[9,1],[4,8],[4,2],[5,2],[2,5],[2,5],[3,5],[2,9],[9,0],[5,4],[5,9],[8,5],[8,7],[7,6],[3,0],[0,2],[8,4],[6,5],[2,8],[7,1],[6,3],[1,0],[6,9],[5,8],[7,1],[6,0],[0,9],[3,4],[6,7],[4,9],[5,3],[5,2],[9,5],[2,8],[2,7],[0,2],[4,3],[6,7],[7,5],[5,3],[2,1],[8,0],[7,6],[4,7],[0,7],[4,1],[9,3],[7,1],[3,2],[8,0],[5,4],[5,0],[2,9],[6,8],[8,1],[0,9],[2,0],[2,1],[0,7],[3,1],[6,7],[7,9],[0,7],[2,7],[4,9],[0,8],[5,1],[6,9],[6,0],[6,1],[8,7],[7,5],[4,8],[1,7],[2,8],[3,2],[9,2],[1,0],[7,2],[0,5],[9,7],[9,8],[1,5],[2,7],[9,3],[4,8],[4,6],[4,3],[1,8],[6,2],[0,7],[6,0],[0,1],[2,8],[1,3],[0,8],[1,7],[5,8],[6,2],[8,3],[3,1],[7,5],[8,6],[6,7],[1,5],[4,3],[1,5],[2,6],[7,2],[4,3],[1,7],[4,5],[4,6],[0,7],[3,9],[5,9],[0,5],[1,8],[2,1],[7,9],[1,6],[9,8],[6,5],[9,7],[4,0],[4,1],[6,2],[0,4],[2,6],[8,5],[1,0],[3,9],[8,0],[3,5],[4,9],[5,8],[9,0],[7,9],[6,9],[9,4],[2,4],[4,0],[0,6],[5,9],[1,7],[5,2],[0,8],[3,9],[1,0],[0,4],[3,9],[5,2],[3,6],[8,5],[1,2],[3,9],[4,2],[0,1],[6,9],[6,2],[6,3],[0,2],[1,6],[9,3],[7,3],[9,1],[5,8],[5,1],[5,4],[5,9],[6,9],[0,8],[3,8],[2,5],[6,2],[1,5],[5,4],[3,9],[9,8],[8,3],[7,3],[3,7],[7,9],[0,1],[5,7],[2,5],[5,9],[7,6],[8,3],[8,4],[0,7],[8,1],[5,6],[0,1],[6,3],[2,5],[2,9],[3,1],[1,6],[4,1],[5,0],[9,7],[9,4],[8,6],[7,9],[2,0],[8,7],[8,7],[8,6],[0,1],[1,8],[3,6],[9,1],[5,9],[1,4],[3,4],[3,5],[9,6],[6,8],[6,4],[5,8],[4,0],[1,5],[5,7],[4,2],[7,9],[1,7],[2,6],[0,5],[7,0],[3,5],[4,6],[2,3],[3,7],[5,8],[9,8],[7,6],[3,1],[5,8],[8,7],[9,1],[5,2],[7,5],[1,6],[8,4],[4,8],[2,8],[2,3],[5,3],[4,6],[6,9],[4,2],[3,1],[2,0],[0,7],[8,1],[2,5],[6,0],[1,3],[6,2],[0,9],[9,7],[7,4],[4,8],[0,2],[8,2],[6,5],[9,1],[9,7],[0,4],[0,5],[9,1],[3,6],[9,4],[4,3],[7,1],[5,6],[3,4],[7,4],[9,7],[5,6],[3,8],[2,1],[7,6],[4,7],[5,3],[6,8],[3,7],[0,1],[7,4],[7,0],[3,1],[2,3],[5,8],[6,4],[8,2],[8,1],[6,9],[4,1],[8,9],[0,8],[7,1],[0,4],[4,0],[9,6],[2,8],[6,9],[5,3],[4,5],[2,1],[5,8],[6,8],[5,3],[0,6],[8,7],[4,5],[5,8],[5,3],[5,7],[6,8],[5,6],[4,5],[3,0],[3,7],[8,9],[7,4],[5,7],[8,7],[9,2],[4,5],[6,8],[9,5],[1,5],[0,8],[3,5],[0,6],[7,4],[3,6],[7,1],[2,7],[0,3],[1,3],[2,5],[8,3],[9,3],[9,1],[0,8],[0,5],[7,1],[5,1],[7,3],[6,5],[6,9],[5,8],[3,6],[9,8],[3,7],[8,0],[8,0],[8,1],[6,4],[1,0],[6,7],[4,5],[4,5],[3,2],[4,8],[5,6],[6,2],[1,6],[3,0],[5,4],[5,8],[0,9],[3,5],[3,0],[9,4],[0,8],[7,0],[3,8],[8,5],[3,9],[5,4],[2,4],[2,9],[8,1],[0,8],[7,8],[6,1],[9,2],[9,6],[6,4],[9,2],[0,4],[8,4],[6,8],[1,7],[0,9],[7,5],[9,7],[4,5],[1,8],[5,8],[6,4],[6,4],[8,3],[9,2],[2,7],[7,9],[8,9],[1,8],[9,6],[7,8],[0,2],[9,7],[9,5],[2,6],[5,0],[0,8],[4,1],[5,2],[3,9],[9,1],[0,4],[8,3],[4,9],[0,4],[7,1],[3,6],[3,0],[7,3],[2,6],[2,9],[8,0],[6,0],[7,5],[6,9],[2,4],[9,2],[5,3],[5,3],[0,4],[5,1],[3,6],[4,7],[4,2],[4,5],[3,2],[0,8],[2,1],[6,1],[9,5],[5,6],[3,9],[8,0],[2,6],[6,9],[1,7],[3,5],[8,4],[6,7],[7,6],[3,1],[5,3],[1,3],[4,6],[4,9],[9,1],[7,4],[9,2],[4,1],[7,1],[5,6],[4,6],[1,7],[1,3],[3,8],[8,6],[4,2],[7,9],[6,8],[3,2],[8,9],[5,6],[2,8],[3,0],[2,3],[5,1],[0,7],[0,3],[9,1],[5,4],[1,6],[4,7],[6,8],[8,0],[4,8],[2,8],[0,3],[8,1],[4,6],[8,9],[6,2],[6,5],[5,6],[1,6],[5,6],[1,5],[3,4],[4,1],[5,1]],[[5,0],[0,6],[3,9],[0,1],[3,0],[5,7],[7,9],[7,1],[2,9],[5,0],[2,1],[4,6],[5,6],[8,6],[3,6],[1,3],[7,4],[4,3],[5,0],[5,8],[8,1],[7,3],[1,7],[5,1],[1,9],[8,9],[4,2],[4,5],[8,0],[8,5],[6,2],[7,2],[9,7],[1,4],[5,1],[8,3],[1,2],[6,9],[0,2],[5,2],[3,0],[9,2],[9,6],[3,5],[3,0],[4,3],[6,0],[1,8],[6,9],[2,6],[9,5],[6,2],[1,3],[3,1],[4,0],[3,5],[7,8],[9,2],[5,4],[9,6],[2,5],[6,7],[0,6],[9,7],[9,2],[4,5],[8,6],[1,8],[2,1],[6,4],[9,3],[2,4],[0,8],[0,4],[9,4],[5,0],[0,9],[5,6],[3,5],[2,7],[6,0],[5,2],[6,2],[1,9],[3,0],[5,9],[3,0],[1,0],[5,6],[0,4],[3,9],[6,2],[2,7],[9,1],[7,8],[4,0],[2,5],[4,8],[4,5],[6,5],[8,4],[5,4],[5,3],[8,2],[8,4],[0,7],[1,4],[8,5],[8,9],[9,2],[8,7],[8,1],[2,8],[0,9],[5,9],[3,0],[7,2],[0,8],[5,8],[1,2],[9,5],[8,3],[3,6],[8,2],[6,0],[1,2],[5,9],[8,7],[6,3],[9,7],[6,7],[5,3],[5,6],[8,3],[0,7],[0,9],[1,7],[8,9],[4,0],[8,4],[2,6],[3,0],[7,9],[7,5],[3,4],[1,2],[6,0],[5,7],[7,0],[2,9],[8,0],[8,2],[2,0],[2,5],[5,4],[7,6],[1,8],[7,5],[8,5],[4,1],[5,2],[5,1],[7,0],[1,5],[3,1],[9,1],[4,3],[8,5],[1,8],[4,5],[4,8],[0,1],[6,5],[4,1],[4,6],[2,3],[6,3],[3,1],[3,6],[5,2],[7,3],[5,2],[0,6],[9,0],[6,7],[0,9],[4,9],[0,3],[1,8],[9,8],[0,4],[1,8],[8,3],[5,8],[4,2],[2,3],[8,5],[3,5],[6,8],[8,0],[4,9],[4,2],[3,7],[8,4],[2,0],[4,0],[8,2],[4,0],[9,8],[4,1],[4,1],[4,3],[3,9],[1,6],[3,6],[4,7],[6,0],[5,0],[3,5],[9,5],[7,5],[7,6],[4,1],[7,0],[6,8],[4,6],[6,7],[0,4],[9,3],[1,7],[5,7],[9,5],[3,7],[6,7],[4,1],[0,5],[3,9],[3,7],[9,5],[2,6],[6,0],[1,7],[3,2],[8,1],[3,2],[2,3],[3,4],[9,2],[6,0],[7,2],[5,4],[5,1],[1,6],[1,8],[7,8],[7,3],[0,8],[5,0],[2,8],[4,2],[1,8],[4,3],[6,9],[7,9],[8,9],[7,5],[7,5],[9,1],[9,1],[7,6],[2,5],[5,7],[4,6],[8,2],[1,6],[5,6],[5,9],[7,6],[5,2],[2,1],[7,8],[7,3],[1,5],[4,7],[3,2],[8,4],[9,2],[8,7],[2,7],[5,8],[9,6],[8,4],[0,9],[1,3],[6,7],[7,2],[6,0],[6,0],[8,2],[0,1],[4,2],[0,2],[7,4],[9,6],[6,1],[5,0],[2,0],[8,9],[1,4],[0,7],[0,2],[5,7],[6,1],[2,9],[4,2],[6,7],[2,7],[5,3],[5,3],[6,8],[3,6],[7,9],[3,5],[3,9],[3,8],[9,4],[8,7],[6,1],[0,6],[8,7],[7,2],[4,6],[5,4],[7,8],[7,8],[9,6],[1,0],[5,6],[2,4],[2,5],[5,6],[9,0],[5,1],[6,7],[9,3],[6,9],[3,4],[5,1],[3,7],[4,7],[0,7],[1,4],[9,0],[2,0],[1,8],[7,6],[3,1],[0,2],[5,6],[4,8],[5,9],[6,5],[5,4],[5,9],[1,4],[6,1],[7,8],[8,6],[8,2],[8,1],[1,8],[8,2],[6,7],[3,1],[5,7],[0,1],[0,7],[9,1],[4,0],[9,2],[5,2],[2,8],[2,3],[4,2],[6,8],[3,8],[6,9],[4,1],[5,9],[3,7],[3,7],[9,3],[6,4],[3,7],[2,6],[0,5],[8,7],[5,4],[3,8],[9,2],[7,6],[7,3],[7,6],[9,4],[9,0],[8,5],[5,7],[2,3],[9,7],[2,1],[3,1],[1,5],[2,5],[4,6],[0,9],[7,3],[6,7],[1,8],[7,8],[7,6],[0,5],[6,0],[6,4],[0,1],[3,4],[7,2],[5,6],[5,2],[9,1],[0,7],[3,8],[5,4],[0,3],[6,9],[9,6],[3,8],[6,5],[8,0],[7,9],[1,0],[5,6],[5,0],[5,4],[9,0],[6,2],[3,7],[7,5],[7,0],[9,2],[2,4],[8,1],[0,1],[7,1],[0,5],[2,8],[8,5],[4,9],[2,9],[5,1],[7,0],[5,2],[5,3],[7,9],[4,8],[6,8],[3,1],[9,4],[5,7],[4,5],[0,4],[3,5],[8,2],[8,6],[9,7],[4,6],[3,7],[2,4],[1,6],[0,1],[4,9],[8,5],[8,4],[6,5],[0,7],[0,2],[4,9],[4,7],[5,7],[4,5],[8,3],[8,2],[0,1],[8,4],[8,9],[3,6],[0,3],[4,9],[8,9],[0,8],[8,6],[4,5],[3,2],[1,6],[2,5],[2,6],[9,7],[0,4],[8,9],[4,2],[3,1],[4,1],[2,4]],[[5,2],[4,6],[6,2],[2,3],[3,6],[6,7],[1,7],[7,8],[9,5],[6,2],[9,8],[3,7],[0,6],[1,2],[9,1],[3,2],[5,7],[4,5],[3,5],[7,2],[1,0],[5,8],[3,8],[5,2],[9,2],[5,6],[5,3],[3,0],[0,6],[0,5],[0,7],[6,9],[0,9],[9,5],[3,5],[1,5],[9,3],[0,2],[0,1],[1,8],[7,5],[6,1],[7,6],[4,6],[6,3],[2,8],[4,2],[5,9],[0,6],[8,0],[4,8],[1,8],[5,1],[3,2],[3,8],[5,6],[7,0],[5,9],[0,8],[8,9],[4,8],[9,2],[8,7],[4,7],[1,8],[5,3],[0,1],[2,1],[1,9],[7,6],[6,1],[5,4],[5,7],[1,9],[9,7],[4,2],[6,4],[6,3],[0,3],[4,8],[8,6],[9,2],[7,1],[4,6],[6,0],[6,5],[8,7],[7,0],[1,6],[0,5],[6,8],[5,7],[3,4],[8,7],[4,6],[8,5],[1,0],[1,5],[5,2],[2,1],[4,0],[0,4],[6,2],[6,7],[4,9],[7,0],[9,0],[7,0],[3,0],[2,0],[9,1],[5,0],[1,5],[4,0],[9,2],[5,8],[8,3],[3,4],[6,3],[6,3],[7,9],[5,1],[8,3],[1,5],[1,2],[3,5],[8,7],[4,5],[9,0],[4,6],[2,6],[1,5],[2,0],[8,6],[2,5],[4,0],[8,9],[7,8],[5,8],[3,4],[6,0],[6,0],[0,7],[3,2],[2,4],[0,9],[2,1],[1,0],[2,6],[9,6],[2,6],[7,5],[2,7],[0,1],[6,1],[9,1],[2,8],[0,2],[6,2],[1,2],[9,8],[5,2],[8,2],[5,7],[0,4],[3,1],[1,7],[4,5],[8,7],[3,7],[9,7],[6,2],[1,9],[6,4],[0,2],[1,5],[2,6],[6,0],[4,1],[1,4],[2,9],[4,8],[6,1],[7,9],[7,2],[3,0],[5,9],[0,4],[3,4],[9,3],[1,7],[5,6],[1,2],[0,6],[5,1],[9,7],[9,1],[7,0],[4,6],[7,0],[1,9],[1,9],[0,5],[0,7],[5,7],[7,2],[9,0],[4,1],[9,7],[7,6],[2,0],[9,4],[9,1],[2,6],[8,3],[9,6],[2,7],[8,9],[6,8],[4,7],[3,4],[2,4],[4,8],[2,9],[7,1],[8,0],[2,4],[0,8],[7,0],[7,2],[3,5],[5,7],[4,1],[7,9],[1,9],[2,9],[7,2],[2,0],[2,0],[7,4],[6,7],[4,1],[3,2],[7,2],[1,8],[8,1],[2,1],[3,1],[9,0],[0,8],[9,8],[4,9],[0,4],[3,5],[5,9],[7,4],[0,2],[7,2],[2,4],[2,3],[0,2],[9,2],[0,7],[6,5],[5,2],[3,5],[4,7],[0,7],[6,4],[8,6],[4,3],[4,3],[2,0],[2,7],[6,2],[4,5],[4,9],[0,9],[6,5],[3,2],[1,6],[4,7],[0,4],[8,6],[4,3],[8,3],[6,1],[4,9],[4,8],[7,1],[9,8],[5,4],[5,2],[3,9],[7,1],[5,9],[9,0],[0,4],[3,7],[9,3],[5,1],[7,5],[2,5],[9,5],[4,7],[9,1],[1,6],[8,0],[6,5],[1,2],[2,5],[4,6],[6,9],[8,3],[3,5],[9,7],[4,8],[9,1],[6,2],[3,9],[1,8],[3,8],[1,7],[7,2],[3,7],[6,5],[1,0],[7,6],[0,2],[8,0],[0,9],[3,5],[6,5],[9,1],[8,4],[1,4],[4,7],[3,7],[6,2],[3,1],[2,8],[0,6],[2,5],[0,3],[3,7],[0,9],[9,8],[5,7],[4,9],[5,6],[8,1],[1,0],[7,2],[1,7],[7,4],[4,7],[4,6],[8,6],[3,2],[5,8],[1,2],[5,6],[5,8],[8,3],[5,0],[5,7],[4,2],[2,7],[6,5],[1,8],[6,4],[5,6],[5,8],[2,7],[1,0],[5,2],[3,6],[0,5],[5,7],[4,7],[4,8],[6,2],[9,3],[5,9],[1,7],[6,7],[1,0],[3,5],[9,0],[8,7],[7,4],[6,1],[5,7],[3,1],[5,3],[1,9],[0,1],[6,4],[6,2],[7,0],[6,2],[5,0],[3,7],[0,5],[9,5],[7,2],[6,8],[2,3],[6,9],[9,1],[2,3],[7,4],[6,5],[0,1],[8,3],[5,1],[0,7],[8,0],[4,6],[8,1],[1,0],[1,4],[8,6],[5,2],[2,1],[8,5],[3,8],[0,4],[9,4],[0,7],[8,1],[8,9],[2,3],[2,9],[6,1],[5,3],[1,7],[1,5],[5,1],[6,9],[1,4],[8,9],[2,0],[4,7],[8,2],[8,9],[2,9],[0,3],[1,0],[3,7],[1,4],[2,7],[7,1],[7,8],[1,0],[9,6],[0,8],[2,5],[5,9],[3,9],[7,4],[3,4],[7,8],[1,5],[2,1],[8,5],[2,0],[9,1],[6,1],[0,7],[8,5],[5,7],[1,8],[3,2],[0,4],[8,2],[8,7],[8,5],[6,1],[5,8],[8,3],[3,6],[9,3],[9,1],[4,7],[5,8],[4,1],[9,7],[1,7],[4,8],[4,6],[4,6],[4,1],[3,9],[6,3],[8,3],[0,7],[8,3],[6,9],[6,1],[4,5],[6,2],[6,8],[1,8],[4,2],[0,5],[9,3],[7,8],[2,7],[1,5],[2,3],[9,0]],[[6,0],[6,7],[2,9],[0,7],[6,8],[0,3],[0,9],[4,8],[5,2],[1,0],[5,9],[1,3],[2,4],[1,8],[3,1],[4,2],[7,1],[6,9],[2,7],[3,0],[2,7],[8,2],[8,4],[8,9],[7,8],[8,9],[5,0],[5,3],[7,2],[8,9],[0,5],[8,3],[1,9],[6,1],[0,9],[7,8],[3,4],[7,8],[4,9],[8,5],[7,1],[4,6],[9,1],[9,4],[2,6],[8,7],[5,3],[6,5],[0,1],[5,2],[3,8],[9,2],[9,7],[7,0],[9,5],[6,2],[4,5],[9,6],[0,8],[0,4],[4,3],[8,0],[1,4],[7,4],[0,3],[5,0],[3,6],[5,9],[1,4],[3,7],[3,1],[3,6],[8,1],[2,9],[3,5],[5,8],[3,1],[6,4],[9,2],[3,1],[3,5],[3,0],[8,0],[1,9],[1,5],[5,9],[8,1],[2,6],[9,5],[5,1],[2,9],[4,8],[3,9],[2,4],[7,6],[0,8],[2,0],[7,9],[6,5],[2,0],[5,7],[5,7],[1,0],[5,9],[7,0],[5,4],[5,7],[1,6],[9,3],[5,3],[6,5],[8,3],[7,1],[2,5],[8,9],[0,3],[6,9],[8,7],[9,2],[2,4],[0,2],[9,7],[9,4],[0,9],[2,0],[7,1],[4,5],[5,2],[5,2],[2,0],[3,7],[4,5],[2,1],[1,3],[6,7],[9,6],[4,6],[6,0],[9,1],[8,1],[3,0],[7,6],[9,1],[2,0],[4,8],[2,5],[1,4],[0,3],[0,8],[4,6],[6,0],[9,2],[1,7],[4,6],[5,4],[0,1],[3,9],[3,4],[9,0],[4,2],[0,8],[8,1],[0,2],[4,8],[7,2],[1,6],[2,1],[1,5],[9,8],[7,6],[2,4],[1,2],[1,3],[1,7],[0,6],[2,5],[4,3],[7,2],[3,8],[0,1],[3,1],[9,8],[4,0],[7,5],[0,7],[0,4],[0,4],[9,5],[5,2],[3,1],[7,4],[0,5],[7,1],[2,5],[7,6],[4,6],[6,4],[7,8],[1,7],[1,0],[7,3],[2,0],[5,7],[5,2],[4,3],[0,4],[0,6],[0,3],[8,3],[7,6],[4,6],[6,2],[3,6],[5,0],[5,4],[9,7],[0,5],[2,5],[0,6],[5,3],[6,2],[5,1],[7,9],[1,5],[5,4],[2,4],[7,0],[9,7],[8,3],[9,4],[4,3],[1,2],[3,8],[4,9],[0,3],[8,0],[3,4],[2,9],[5,1],[3,2],[5,7],[4,2],[5,1],[6,0],[4,8],[5,4],[1,9],[7,3],[1,9],[1,3],[7,6],[0,8],[6,4],[6,4],[9,6],[0,4],[4,5],[3,1],[5,0],[4,8],[1,4],[9,8],[5,2],[7,3],[0,5],[8,9],[4,6],[7,3],[3,2],[3,7],[9,0],[3,4],[0,1],[7,0],[8,7],[1,6],[9,6],[5,1],[4,3],[5,0],[0,3],[4,5],[7,8],[6,9],[7,1],[6,5],[3,4],[4,5],[3,7],[7,8],[4,7],[4,0],[2,5],[3,9],[7,2],[8,0],[2,4],[8,0],[2,7],[0,4],[0,3],[5,0],[8,1],[4,0],[1,7],[9,1],[8,9],[1,3],[6,7],[8,9],[7,0],[5,6],[6,8],[8,7],[1,2],[6,8],[5,7],[2,8],[0,7],[1,6],[1,4],[3,9],[6,3],[9,2],[8,3],[4,0],[3,6],[7,5],[5,6],[1,5],[5,1],[9,0],[5,2],[0,9],[4,3],[0,1],[2,0],[1,9],[3,9],[6,3],[7,9],[6,1],[1,3],[7,1],[2,0],[0,3],[8,9],[0,2],[7,4],[4,0],[9,7],[4,8],[5,7],[5,2],[0,9],[6,0],[7,2],[4,6],[8,2],[5,8],[8,3],[9,5],[2,1],[6,9],[4,3],[6,0],[2,6],[1,4],[5,6],[0,7],[7,2],[6,4],[2,9],[9,5],[8,0],[1,3],[0,9],[4,7],[5,2],[5,6],[0,7],[6,8],[9,6],[0,9],[8,2],[8,2],[9,1],[5,0],[6,8],[4,5],[6,4],[8,5],[3,7],[5,7],[0,2],[5,2],[2,0],[8,3],[6,7],[2,7],[5,4],[0,3],[8,7],[2,3],[2,8],[2,3],[1,4],[8,5],[7,6],[6,4],[8,9],[7,3],[9,3],[3,2],[3,2],[7,8],[2,4],[6,7],[1,6],[7,5],[4,6],[5,7],[6,3],[8,0],[0,4],[5,3],[9,7],[3,0],[9,8],[9,4],[1,7],[1,3],[6,5],[6,2],[2,6],[2,5],[9,7],[3,1],[7,6],[5,9],[0,5],[6,4],[1,5],[5,4],[1,3],[2,3],[0,8],[5,6],[8,5],[5,3],[1,4],[1,8],[9,7],[8,3],[3,2],[3,9],[3,2],[1,0],[0,2],[4,9],[4,7],[7,5],[3,6],[5,6],[0,9],[0,6],[9,8],[9,7],[9,4],[5,4],[2,3],[1,5],[2,6],[6,1],[2,0],[8,3],[7,4],[3,0],[2,6],[4,8],[8,0],[6,4],[8,9],[1,2],[6,3],[6,5],[4,7],[2,8],[4,7],[8,9],[6,3],[9,4],[0,7],[3,2],[0,7],[7,2],[8,2],[2,3],[6,2],[3,6],[3,9],[0,7],[0,8],[9,2],[8,7],[5,3],[4,1],[7,2],[2,7],[1,4],[8,3],[7,3]],[[9,4],[3,5],[5,6],[0,8],[9,8],[4,2],[2,7],[0,5],[4,9],[2,6],[9,8],[9,8],[1,4],[5,8],[8,4],[5,0],[4,7],[8,4],[1,3],[5,2],[9,1],[5,6],[1,4],[6,0],[1,5],[9,6],[1,0],[3,4],[8,1],[9,5],[8,2],[3,6],[2,3],[4,2],[8,0],[2,5],[3,5],[3,9],[0,2],[6,9],[4,0],[4,0],[3,1],[1,0],[0,5],[2,5],[3,0],[6,5],[8,0],[9,3],[8,7],[7,8],[9,7],[0,2],[6,2],[2,7],[8,7],[5,2],[8,1],[0,4],[4,6],[4,1],[8,7],[8,3],[1,2],[7,6],[4,2],[8,0],[0,2],[7,5],[3,6],[7,3],[5,1],[5,1],[8,4],[7,0],[2,4],[4,7],[8,1],[4,7],[7,4],[0,9],[1,7],[3,5],[5,0],[1,8],[0,7],[3,5],[5,0],[7,2],[9,5],[9,8],[5,7],[8,0],[4,5],[3,0],[6,0],[6,8],[1,6],[6,3],[3,7],[6,5],[6,9],[5,4],[8,4],[8,6],[6,4],[2,8],[3,5],[2,8],[3,7],[5,7],[3,5],[6,8],[1,4],[6,3],[8,2],[1,0],[7,2],[9,7],[3,9],[1,6],[2,5],[7,3],[6,8],[9,2],[5,0],[3,7],[5,4],[3,1],[0,8],[7,2],[5,4],[6,7],[5,2],[9,2],[2,7],[3,7],[8,0],[4,6],[2,4],[3,1],[8,9],[2,5],[1,3],[6,4],[0,3],[0,6],[0,7],[6,1],[2,5],[5,0],[3,7],[7,2],[2,6],[9,7],[2,1],[0,3],[0,4],[2,1],[9,3],[2,8],[2,9],[1,8],[3,7],[7,4],[6,9],[3,2],[9,8],[7,3],[2,5],[1,5],[6,9],[4,8],[1,2],[9,0],[1,6],[8,6],[8,2],[8,7],[8,4],[6,0],[6,3],[5,6],[8,2],[2,1],[4,0],[4,7],[7,4],[0,1],[8,1],[0,7],[6,2],[6,8],[4,9],[1,7],[4,8],[2,4],[6,3],[0,5],[5,6],[5,6],[9,4],[2,3],[4,3],[9,7],[5,9],[3,4],[0,4],[2,1],[5,2],[5,9],[9,5],[1,2],[6,4],[7,4],[1,7],[9,4],[5,2],[0,9],[0,3],[5,3],[4,6],[5,9],[5,0],[5,4],[6,3],[7,2],[4,5],[3,4],[4,9],[3,0],[5,9],[9,8],[1,4],[7,4],[7,9],[0,6],[4,1],[0,8],[8,2],[5,0],[2,6],[5,7],[7,0],[5,6],[7,5],[3,8],[0,1],[0,8],[4,2],[5,8],[5,3],[0,6],[7,2],[9,7],[1,5],[3,0],[7,1],[3,5],[1,8],[7,8],[8,5],[1,7],[1,7],[0,9],[3,8],[6,5],[5,1],[8,7],[4,5],[9,0],[3,6],[0,2],[9,6],[1,2],[7,3],[0,3],[3,1],[3,9],[8,5],[4,8],[9,0],[8,7],[5,4],[4,8],[3,4],[7,2],[8,3],[8,2],[0,1],[0,9],[7,9],[1,5],[2,7],[3,6],[8,1],[2,7],[4,6],[0,2],[9,8],[4,7],[0,1],[9,0],[1,7],[4,3],[7,0],[9,2],[1,7],[0,6],[9,7],[1,0],[2,3],[9,6],[6,4],[4,7],[9,3],[1,0],[9,5],[7,1],[0,5],[6,5],[1,0],[2,5],[8,0],[5,4],[0,5],[0,9],[9,1],[1,2],[1,8],[5,4],[8,5],[3,8],[1,5],[5,2],[8,6],[8,2],[4,1],[4,7],[7,4],[1,7],[5,7],[4,0],[6,4],[1,6],[8,5],[4,8],[7,1],[0,4],[7,5],[5,3],[8,2],[8,0],[1,7],[9,2],[7,5],[4,0],[2,0],[9,1],[6,1],[1,6],[5,1],[3,5],[5,2],[6,7],[9,4],[8,9],[3,6],[1,3],[0,6],[1,8],[3,2],[5,6],[3,4],[4,7],[2,4],[4,8],[8,9],[0,1],[4,1],[1,9],[5,6],[7,6],[5,7],[2,4],[5,4],[2,1],[0,3],[3,7],[7,8],[5,3],[3,1],[2,8],[7,9],[9,4],[0,3],[6,1],[9,4],[6,4],[6,0],[4,9],[3,2],[0,2],[2,8],[0,4],[7,6],[9,0],[2,1],[7,4],[0,7],[1,2],[3,2],[9,0],[1,8],[7,3],[8,1],[6,3],[4,1],[5,4],[6,1],[7,0],[3,8],[9,8],[7,4],[0,1],[1,8],[5,6],[7,2],[5,8],[8,7],[9,4],[8,2],[3,4],[2,1],[6,8],[3,8],[2,8],[3,9],[0,4],[7,4],[0,9],[0,1],[4,3],[5,7],[5,4],[6,0],[2,7],[3,6],[0,1],[3,7],[3,8],[0,3],[5,1],[2,0],[9,0],[2,1],[7,2],[6,0],[0,6],[7,3],[2,4],[8,1],[9,0],[2,3],[1,9],[2,4],[6,5],[9,2],[9,2],[0,7],[6,5],[0,5],[1,0],[7,5],[9,1],[0,6],[7,1],[8,3],[6,8],[2,0],[2,6],[2,5],[8,5],[6,9],[8,9],[4,5],[9,7],[8,9],[1,7],[8,7],[2,4],[1,7],[6,9],[1,0],[4,6],[4,3],[6,7],[3,9],[7,0],[9,8],[5,6],[4,1],[9,3],[9,3],[9,6],[4,8],[8,2],[6,8],[4,9],[4,3],[3,1]],[[8,4],[8,7],[3,0],[4,6],[8,2],[3,2],[0,7],[8,6],[9,5],[8,5],[7,3],[5,8],[0,2],[5,2],[5,8],[0,8],[6,7],[8,2],[7,5],[9,4],[0,8],[0,5],[8,6],[4,0],[3,0],[3,6],[6,8],[3,4],[6,1],[3,9],[7,6],[0,4],[6,5],[7,9],[1,0],[1,8],[0,5],[0,9],[4,3],[0,1],[8,3],[9,6],[0,4],[6,5],[5,7],[7,2],[6,8],[7,0],[7,8],[9,1],[6,4],[1,2],[5,3],[2,0],[3,0],[6,7],[4,0],[6,0],[9,2],[7,5],[9,8],[8,4],[7,9],[5,7],[5,1],[2,8],[5,7],[8,6],[2,0],[1,9],[3,9],[0,8],[2,1],[7,2],[6,1],[8,7],[0,2],[0,2],[5,2],[8,7],[1,6],[7,8],[1,9],[6,3],[9,0],[8,1],[6,7],[0,6],[7,6],[9,4],[0,9],[7,5],[7,2],[4,0],[1,9],[5,7],[2,3],[8,7],[9,0],[6,5],[4,8],[4,9],[1,0],[4,1],[5,7],[8,3],[3,9],[4,8],[6,3],[6,1],[5,6],[7,5],[7,6],[2,7],[9,3],[6,4],[9,5],[8,6],[2,4],[4,8],[2,6],[4,5],[7,6],[6,5],[7,2],[9,6],[6,2],[7,4],[1,2],[8,1],[7,8],[4,6],[2,6],[1,8],[2,3],[5,9],[4,2],[1,0],[7,1],[7,4],[2,8],[4,3],[7,2],[8,5],[8,2],[0,1],[9,0],[3,9],[8,7],[5,3],[2,7],[2,3],[3,6],[0,8],[1,4],[5,8],[9,3],[9,5],[4,3],[6,1],[4,6],[6,4],[0,1],[5,7],[3,2],[3,0],[6,9],[9,1],[6,0],[1,0],[8,4],[8,5],[8,9],[3,2],[4,9],[3,6],[3,7],[7,5],[8,1],[1,3],[7,1],[2,7],[5,1],[5,0],[7,0],[6,0],[3,1],[2,1],[1,5],[1,4],[1,8],[0,6],[9,6],[9,6],[6,8],[4,7],[4,9],[3,0],[7,9],[7,4],[3,9],[5,3],[4,0],[1,8],[2,3],[7,3],[6,9],[2,0],[0,1],[7,6],[9,4],[8,9],[0,9],[0,8],[4,2],[1,3],[1,0],[1,6],[0,9],[4,2],[4,2],[2,5],[0,4],[0,5],[7,9],[9,0],[7,8],[3,8],[8,6],[9,0],[5,6],[7,8],[2,6],[2,4],[0,4],[5,9],[1,8],[2,4],[1,0],[3,4],[7,1],[7,6],[4,5],[5,6],[1,8],[2,9],[8,0],[5,4],[2,8],[9,3],[7,6],[2,5],[1,0],[4,5],[6,9],[7,2],[6,2],[0,6],[7,2],[4,5],[0,4],[3,6],[2,0],[1,4],[6,0],[6,8],[7,2],[2,3],[8,7],[2,7],[5,3],[4,9],[5,2],[6,3],[3,0],[8,2],[7,4],[7,9],[5,6],[3,6],[0,5],[1,0],[8,1],[1,6],[8,1],[3,4],[8,7],[1,3],[8,5],[6,2],[1,2],[7,3],[2,3],[1,2],[0,8],[5,9],[7,9],[0,8],[3,1],[4,9],[5,3],[2,9],[5,4],[4,1],[8,9],[4,0],[7,3],[3,1],[6,3],[4,9],[3,2],[5,1],[5,2],[9,5],[5,8],[0,8],[1,5],[7,8],[3,4],[9,5],[9,4],[4,0],[8,4],[4,5],[6,1],[8,0],[4,9],[0,7],[2,4],[7,1],[0,8],[3,0],[3,2],[8,7],[2,1],[0,4],[9,2],[4,9],[1,4],[7,4],[3,6],[1,5],[8,5],[1,9],[3,6],[6,1],[1,3],[8,3],[3,2],[3,9],[4,1],[8,5],[6,3],[8,4],[7,2],[8,2],[1,3],[1,0],[8,0],[7,4],[6,1],[3,4],[8,3],[6,2],[6,2],[5,3],[7,4],[1,4],[7,8],[2,6],[8,2],[2,1],[7,5],[6,5],[9,5],[8,3],[9,5],[1,0],[4,8],[5,4],[7,8],[9,4],[5,1],[0,3],[7,9],[5,1],[5,6],[5,9],[6,4],[2,5],[1,4],[0,9],[5,7],[8,9],[0,1],[7,6],[4,8],[7,6],[2,3],[1,3],[2,0],[3,7],[5,4],[1,9],[9,5],[1,2],[2,0],[0,6],[4,2],[8,4],[0,9],[4,9],[8,0],[2,5],[7,8],[4,6],[7,1],[1,9],[4,2],[6,1],[7,4],[2,8],[2,8],[7,9],[1,5],[1,4],[1,7],[3,2],[2,5],[1,2],[2,4],[9,6],[3,9],[5,3],[0,8],[0,8],[1,3],[5,7],[9,8],[3,0],[1,3],[8,3],[0,9],[2,4],[5,4],[8,4],[7,8],[6,1],[1,9],[5,2],[4,7],[3,5],[5,2],[0,1],[2,1],[4,5],[7,5],[8,9],[9,4],[2,7],[1,7],[5,0],[4,6],[6,9],[9,4],[8,3],[8,4],[5,4],[6,7],[1,3],[1,3],[2,4],[8,1],[9,2],[5,0],[8,9],[2,0],[2,5],[6,0],[5,1],[5,2],[8,3],[9,0],[4,1],[2,0],[4,7],[6,9],[8,2],[1,0],[3,2],[1,0],[5,9],[0,5],[7,1],[6,5],[7,1],[9,6],[6,5],[1,8],[5,2],[5,0],[1,0],[0,5],[5,2],[6,2],[4,6],[1,2],[2,9],[3,4],[4,8],[1,0],[2,5]],[[9,5],[8,2],[6,5],[5,4],[3,0],[3,4],[4,6],[6,4],[5,2],[3,1],[7,6],[2,8],[4,5],[2,4],[1,8],[5,7],[7,2],[8,3],[9,1],[5,3],[3,0],[7,5],[0,2],[3,4],[2,9],[6,9],[9,1],[2,5],[2,4],[6,2],[8,7],[8,7],[2,8],[9,4],[2,6],[0,1],[4,0],[3,5],[0,7],[5,2],[9,3],[5,1],[9,8],[3,9],[9,1],[0,6],[7,2],[7,8],[3,4],[7,2],[5,8],[7,9],[2,0],[1,3],[3,2],[3,7],[8,3],[2,8],[8,6],[5,7],[0,2],[4,9],[1,2],[0,9],[6,2],[1,4],[4,9],[1,4],[0,9],[0,5],[0,3],[9,3],[5,9],[4,2],[7,9],[0,4],[9,6],[2,1],[2,9],[9,8],[9,1],[3,7],[2,7],[7,3],[9,6],[2,3],[9,8],[9,7],[6,2],[1,3],[6,3],[4,6],[4,8],[5,6],[8,1],[4,5],[3,8],[2,5],[8,7],[1,4],[9,5],[1,4],[6,3],[4,8],[4,2],[1,6],[0,6],[0,3],[1,9],[6,7],[5,6],[5,9],[5,1],[8,3],[8,5],[3,0],[6,3],[2,0],[6,9],[8,0],[1,9],[0,4],[8,3],[1,0],[7,2],[7,9],[1,0],[6,1],[8,4],[5,7],[8,7],[0,4],[8,9],[4,1],[9,0],[6,0],[2,4],[3,7],[3,1],[1,4],[4,1],[2,9],[5,8],[1,8],[7,2],[5,3],[4,0],[9,3],[2,9],[2,1],[2,1],[6,9],[3,6],[4,7],[1,4],[2,9],[2,4],[1,0],[2,9],[1,6],[6,1],[7,4],[7,6],[5,7],[8,2],[3,8],[0,7],[7,0],[9,4],[2,3],[3,2],[8,7],[5,6],[7,1],[3,0],[8,9],[3,8],[7,2],[0,1],[5,2],[3,4],[0,6],[1,2],[3,0],[4,1],[1,9],[6,0],[8,6],[1,3],[6,0],[9,3],[7,1],[1,3],[7,4],[6,5],[5,7],[1,7],[0,6],[7,8],[9,6],[4,1],[1,2],[1,3],[7,0],[4,0],[7,9],[2,7],[6,7],[0,8],[9,1],[2,5],[7,6],[3,9],[1,8],[0,1],[0,5],[2,4],[4,5],[0,9],[5,9],[7,8],[0,1],[3,8],[7,5],[1,2],[2,3],[2,1],[7,6],[4,2],[2,6],[9,5],[4,6],[4,0],[4,1],[1,3],[2,0],[8,9],[6,1],[1,5],[9,4],[2,1],[6,1],[7,2],[3,4],[4,5],[9,0],[1,2],[9,8],[4,1],[6,8],[1,8],[3,2],[6,9],[8,7],[4,1],[0,1],[2,8],[8,1],[5,9],[6,5],[1,9],[8,2],[2,7],[4,5],[0,5],[8,1],[0,1],[2,1],[5,7],[3,5],[9,5],[2,8],[3,4],[3,5],[7,6],[9,4],[5,8],[2,0],[9,4],[9,2],[9,2],[5,0],[2,6],[9,7],[9,6],[9,0],[2,9],[8,1],[2,7],[3,2],[9,5],[1,9],[2,3],[4,8],[1,7],[3,4],[6,2],[8,5],[0,5],[8,9],[5,0],[7,1],[8,5],[2,1],[3,1],[4,9],[0,2],[3,7],[7,8],[9,7],[7,2],[0,3],[1,5],[2,8],[9,2],[1,6],[0,4],[5,4],[2,7],[1,4],[5,9],[0,1],[3,1],[4,2],[3,7],[6,3],[9,8],[5,8],[6,5],[2,9],[1,8],[4,2],[3,4],[4,8],[8,2],[7,3],[3,9],[6,3],[2,7],[0,8],[7,2],[8,9],[9,5],[8,0],[0,6],[4,1],[9,1],[2,6],[7,6],[4,7],[2,5],[4,0],[6,3],[0,3],[8,7],[7,2],[9,0],[8,6],[0,7],[2,5],[3,2],[7,9],[0,3],[9,6],[8,5],[9,5],[0,1],[5,2],[6,3],[0,8],[1,8],[0,6],[2,7],[0,7],[7,3],[8,6],[1,2],[9,1],[9,6],[9,8],[6,0],[2,7],[4,1],[2,9],[7,3],[6,9],[3,8],[0,7],[5,1],[9,2],[2,8],[6,1],[8,1],[5,6],[5,9],[8,6],[9,2],[6,8],[9,0],[0,8],[1,3],[7,3],[9,2],[7,2],[0,9],[2,3],[3,5],[0,6],[6,0],[4,2],[9,6],[1,3],[6,2],[3,0],[2,5],[9,0],[8,4],[0,2],[9,1],[4,2],[5,4],[7,8],[3,0],[0,7],[3,1],[2,4],[9,1],[7,2],[9,7],[9,5],[1,7],[9,0],[1,2],[8,0],[7,5],[2,1],[8,2],[1,8],[5,0],[3,0],[0,7],[0,2],[0,8],[5,0],[9,1],[7,1],[2,1],[6,4],[4,1],[0,1],[2,4],[7,3],[7,3],[3,7],[6,5],[7,1],[1,8],[2,8],[7,8],[5,6],[3,7],[8,3],[0,6],[5,0],[9,7],[2,3],[3,2],[3,5],[6,1],[9,3],[7,9],[6,3],[7,8],[9,5],[0,9],[5,2],[1,8],[9,4],[6,3],[3,6],[3,4],[3,7],[5,7],[4,7],[3,4],[2,1],[7,1],[0,4],[1,7],[5,2],[5,2],[3,2],[2,5],[4,3],[1,7],[2,1],[5,7],[7,8],[5,7],[0,1],[9,0],[2,1],[0,7],[9,1],[9,6],[5,0],[4,8],[4,7],[3,7],[9,0],[1,8],[4,0]],[[1,5],[2,5],[3,4],[1,5],[0,8],[6,3],[5,3],[5,9],[6,4],[4,7],[7,9],[8,7],[6,1],[3,8],[8,3],[8,3],[5,7],[8,5],[0,9],[6,3],[2,6],[8,5],[6,4],[8,7],[3,7],[5,0],[3,2],[4,9],[7,5],[1,6],[1,8],[2,6],[9,7],[2,4],[4,1],[5,6],[0,6],[7,6],[2,5],[5,1],[4,6],[2,3],[4,9],[7,1],[8,0],[4,8],[9,5],[9,5],[0,4],[2,9],[7,2],[7,1],[4,2],[3,9],[9,3],[2,1],[8,4],[2,3],[0,3],[7,8],[2,8],[9,2],[7,4],[0,3],[8,4],[3,0],[6,1],[3,2],[8,2],[5,0],[1,5],[0,2],[0,7],[5,9],[5,6],[6,9],[5,3],[2,1],[6,0],[4,0],[0,2],[5,6],[7,0],[9,1],[0,5],[3,6],[7,1],[4,1],[0,1],[4,7],[6,5],[2,9],[6,0],[0,4],[3,8],[5,2],[8,4],[6,5],[7,3],[3,2],[8,7],[0,6],[9,4],[9,4],[3,1],[9,6],[3,7],[5,1],[4,1],[7,1],[8,1],[4,7],[9,7],[5,7],[3,6],[1,5],[8,4],[3,2],[7,2],[7,0],[3,6],[4,9],[0,5],[3,6],[6,7],[4,7],[7,0],[5,4],[8,0],[2,0],[7,9],[2,7],[5,0],[6,1],[2,3],[6,7],[8,0],[2,6],[3,7],[0,4],[5,7],[2,7],[7,4],[6,2],[8,5],[2,0],[6,1],[6,2],[4,6],[2,0],[4,7],[7,3],[1,8],[0,9],[3,6],[1,3],[5,6],[3,5],[6,5],[8,4],[6,1],[6,3],[6,8],[5,0],[6,3],[1,7],[5,3],[7,4],[4,9],[8,1],[3,6],[2,8],[5,4],[4,6],[1,9],[2,3],[9,5],[0,9],[6,1],[3,2],[4,6],[4,8],[7,3],[8,1],[0,9],[9,0],[3,4],[9,7],[7,3],[3,2],[9,5],[7,0],[1,6],[3,1],[9,5],[8,6],[3,9],[9,1],[7,5],[7,2],[6,0],[6,0],[6,8],[6,7],[5,7],[3,5],[0,4],[2,6],[7,0],[7,8],[2,0],[9,7],[9,4],[1,8],[0,6],[0,1],[5,3],[2,9],[9,3],[9,6],[7,2],[3,4],[9,8],[5,7],[2,0],[4,3],[6,0],[7,2],[7,2],[0,8],[9,0],[3,2],[5,0],[7,8],[9,3],[6,0],[1,7],[4,7],[7,5],[9,4],[4,3],[6,8],[0,9],[0,5],[2,4],[2,8],[1,0],[5,8],[2,9],[6,2],[2,8],[3,7],[1,0],[8,1],[7,3],[5,1],[7,6],[9,0],[2,7],[3,8],[2,1],[1,9],[3,8],[0,6],[3,2],[0,2],[8,1],[2,0],[2,9],[6,1],[0,9],[3,8],[2,1],[5,7],[9,6],[9,0],[4,5],[5,4],[3,0],[1,9],[2,4],[4,9],[7,4],[7,1],[4,8],[9,4],[2,3],[4,5],[0,9],[2,7],[8,5],[8,0],[3,6],[9,7],[2,3],[8,7],[3,6],[4,8],[2,7],[9,5],[9,0],[7,9],[6,5],[1,5],[9,6],[5,3],[6,5],[7,2],[0,3],[6,9],[2,5],[6,3],[8,7],[6,0],[8,0],[4,9],[3,2],[7,2],[5,6],[6,4],[9,8],[1,9],[5,2],[9,1],[7,6],[0,4],[8,4],[9,4],[1,6],[1,6],[1,9],[4,9],[3,9],[4,8],[9,8],[4,5],[0,4],[0,2],[8,1],[9,5],[2,9],[2,8],[3,5],[3,9],[4,3],[6,4],[5,1],[7,8],[1,0],[0,7],[9,8],[9,3],[6,0],[7,6],[7,3],[0,7],[0,6],[2,9],[5,3],[8,9],[2,9],[4,3],[6,5],[5,2],[0,5],[5,6],[8,7],[4,7],[0,7],[1,4],[9,6],[7,5],[5,2],[3,7],[1,0],[5,8],[9,7],[4,6],[9,3],[3,2],[3,0],[2,6],[6,5],[0,5],[1,5],[1,2],[6,5],[6,2],[6,1],[5,7],[9,8],[8,3],[7,6],[4,7],[1,3],[1,5],[2,1],[8,5],[1,8],[1,5],[1,8],[3,6],[7,6],[4,7],[7,4],[3,1],[1,3],[5,8],[8,0],[8,0],[1,0],[4,9],[3,7],[9,0],[7,9],[2,8],[2,1],[0,9],[4,5],[3,5],[1,4],[2,5],[5,0],[2,6],[4,1],[1,5],[0,3],[0,5],[3,1],[0,5],[6,1],[0,4],[7,5],[3,5],[8,3],[3,5],[1,7],[6,1],[2,3],[4,2],[4,7],[6,8],[4,9],[7,4],[6,1],[9,8],[7,6],[9,7],[9,5],[5,2],[2,8],[6,8],[8,3],[3,8],[1,3],[5,7],[3,2],[3,7],[7,6],[8,1],[0,4],[1,0],[0,2],[8,3],[2,0],[2,8],[9,2],[3,4],[8,6],[2,5],[9,5],[9,1],[5,2],[5,8],[3,8],[0,4],[0,5],[1,0],[4,3],[5,8],[0,3],[3,2],[0,2],[2,5],[5,7],[7,8],[1,8],[6,4],[4,1],[6,7],[0,4],[3,0],[1,7],[8,1],[2,5],[9,1],[8,5],[3,2],[5,7],[8,5],[6,8],[9,2],[6,9],[9,1],[3,1],[1,3],[9,2],[3,8],[5,3],[3,5],[0,7],[4,7]]]
ZW = 1088
def setup_inputs(rng):
    return {"z": rng.standard_normal((N, 128, ZW), dtype=np.float32), "g": rng.random((N, 128, T * K), dtype=np.float32)}
def reference(z, g):
    y = np.zeros((N, 128, T), np.float64)
    fill = [0] * N
    for r in range(N):
        for t in range(T):
            for k, e in enumerate(ROUTE[r][t]):
                y[r][:, t] += g[r][:, t * K + k].astype(np.float64) * z[e][:, fill[e]].astype(np.float64)
                fill[e] += 1
    return {"y": y.astype(z.dtype)}

@@ -1,0 +1,78 @@
+from concourse.mybir import AluOpType
+
+NR = 10
+SCRATCH = {
+    "zs": ("sbuf", [128, 1088], "float32"),
+    "gs": ("sbuf", [128, 1024], "float32"),
+    "land": ("sbuf", [128, 1024], "float32"),
+    "prod": ("sbuf", [128, 1024], "float32"),
+    "ys": ("sbuf", [128, 512], "float32"),
+}
+SEMAPHORES = ["zl", "gl", "sent", "vdone", "added", "stored"] + ["arr%d" % e for e in range(NR)]
+
+
+def _runs(cols):
+    out = []
+    i = 0
+    while i < len(cols):
+        j = i + 1
+        d = 1
+        if j < len(cols):
+            d = cols[j] - cols[i]
+            j += 1
+            while j < len(cols) and cols[j] - cols[j - 1] == d:
+                j += 1
+        out.append((i, j - i, d))
+        i = j
+    return out
+
+
+def rank_program(g, core, T, topo):
+    me = T.rank_of(core)
+    if me is None:
+        return
+    route = T.tables["ROUTE"]
+    K = T.tables["K"]
+    n = len(route)
+    wcols = [[[t * K + k for t in range(len(route[r])) for k in range(K) if route[r][t][k] == e]
+              for r in range(n)] for e in range(n)]
+    cnt = [[len(wcols[e][r]) for r in range(n)] for e in range(n)]
+    zoff = [[sum(cnt[e][:r]) for r in range(n)] for e in range(n)]
+    loff = [[sum(cnt[x][r] for x in range(e)) for r in range(n)] for e in range(n)]
+
+    g.sync.dma_start(T.zs[:], T.z[:]).then_inc(T.sem.zl, 16)
+    g.scalar.dma_start(T.gs[:], T.g[:]).then_inc(T.sem.gl, 16)
+
+    g.wait_ge(T.sem.zl, 16)
+    order = [(me + d) % n for d in range(1, n)]
+    for r in order:
+        dst = T.cores[r]
+        rid, pid, _se = topo.addr(dst)
+        g.remote_dma(T.land[:, loff[me][r]:loff[me][r] + cnt[me][r]],
+                     T.zs[:, zoff[me][r]:zoff[me][r] + cnt[me][r]],
+                     T.sem["arr%d" % me], T.sem.sent, pid, rid, topo.mask(core, dst))
+
+    v = g.vector
+    v.wait_ge(T.sem.gl, 16)
+    v.wait_ge(T.sem.zl, 16)
+    nops = 0
+    for e in [me] + [(me - d) % n for d in range(1, n)]:
+        if e == me:
+            buf, base = T.zs, zoff[me][me]
+        else:
+            buf, base = T.land, loff[e][me]
+            v.wait_ge(T.sem["arr%d" % e], 8)
+        cols = wcols[e][me]
+        for (i, m, d) in _runs(cols):
+            a = cols[i]
+            b = a + (m - 1) * d + 1
+            v.tensor_tensor(T.prod[:, a:b:d], T.gs[:, a:b:d], buf[:, base + i:base + i + m],
+                            AluOpType.mult).then_inc(T.sem.vdone, 1)
+            nops += 1
+    v.wait_ge(T.sem.vdone, nops)
+    v.tensor_tensor(T.ys[:], T.prod[:, 0::2], T.prod[:, 1::2], AluOpType.add).then_inc(T.sem.added, 1)
+
+    g.sync.wait_ge(T.sem.added, 1)
+    g.sync.dma_start(T.y[:], T.ys[:]).then_inc(T.sem.stored, 16)
+    g.sync.wait_ge(T.sem.stored, 16)
+    g.wait_ge(T.sem.sent, 8 * (n - 1))

@@ -1,6 +1,7 @@
 from concourse.mybir import AluOpType
 
 NR = 10
+HELPER = 3
 SCRATCH = {
     "zs": ("sbuf", [128, 1088], "float32"),
     "gs": ("sbuf", [128, 1024], "float32"),
@@ -8,61 +9,126 @@ SCRATCH = {
     "prod": ("sbuf", [128, 1024], "float32"),
     "ys": ("sbuf", [128, 512], "float32"),
 }
-SEMAPHORES = ["zl", "gl", "sent", "vdone", "added", "stored"] + ["arr%d" % e for e in range(NR)]
+SEMAPHORES = ["zl", "gl", "relay", "sent", "vdone", "added", "stored"] + ["arr%d" % e for e in range(NR)]
 
 
 def _runs(cols):
-    out = []
-    i = 0
-    while i < len(cols):
+    n = len(cols)
+    best = [0] + [n + 1] * n
+    prev = [0] * (n + 1)
+    for i in range(n):
         j = i + 1
-        d = 1
-        if j < len(cols):
-            d = cols[j] - cols[i]
+        while True:
+            if best[i] + 1 < best[j]:
+                best[j] = best[i] + 1
+                prev[j] = i
+            if j >= n or (j - i >= 2 and cols[j] - cols[j - 1] != cols[i + 1] - cols[i]):
+                break
             j += 1
-            while j < len(cols) and cols[j] - cols[j - 1] == d:
-                j += 1
-        out.append((i, j - i, d))
-        i = j
-    return out
+    out = []
+    j = n
+    while j > 0:
+        i = prev[j]
+        out.append((i, j - i, cols[i + 1] - cols[i] if j - i > 1 else 1))
+        j = i
+    return out[::-1]
 
 
-def rank_program(g, core, T, topo):
-    me = T.rank_of(core)
-    if me is None:
-        return
-    route = T.tables["ROUTE"]
-    K = T.tables["K"]
+def _plan(route, K):
     n = len(route)
     wcols = [[[t * K + k for t in range(len(route[r])) for k in range(K) if route[r][t][k] == e]
               for r in range(n)] for e in range(n)]
     cnt = [[len(wcols[e][r]) for r in range(n)] for e in range(n)]
     zoff = [[sum(cnt[e][:r]) for r in range(n)] for e in range(n)]
     loff = [[sum(cnt[x][r] for x in range(e)) for r in range(n)] for e in range(n)]
+    pieces = []
+    for e in range(n):
+        m = e ^ 1
+        far = [2, 3, 4, 5] if e % 2 == 0 else [5, 6, 7, 8]
+        near = [6, 7, 8, 9] if e % 2 == 0 else [1, 2, 3, 4]
+        x1 = sum(cnt[e][(e + o) % n] for o in far if o % 2)
+        x0 = sum(cnt[e][(e + o) % n] for o in near if o % 2)
+        h1 = (cnt[e][m] + x0 - x1) // 2
+        h0 = cnt[e][m] - h1
+        p0 = [((e + o) % n, 0, cnt[e][(e + o) % n]) for o in near]
+        p1 = [((e + o) % n, 0, cnt[e][(e + o) % n]) for o in far]
+        if e % 2 == 0:
+            p0 = p0 + [(m, 0, h0)]
+            p1 = [(m, h0, h1)] + p1
+        else:
+            p1 = p1 + [(m, 0, h1)]
+            p0 = [(m, h1, h0)] + p0
+        pieces.append((p0, p1))
+    return wcols, cnt, zoff, loff, pieces
 
-    g.sync.dma_start(T.zs[:], T.z[:]).then_inc(T.sem.zl, 16)
+
+def _send(g, T, topo, core, e, plist, zoff, loff):
+    for (r, s, w) in plist:
+        dst = T.cores[r]
+        rid, pid, _se = topo.addr(dst)
+        g.remote_dma(T.land[:, loff[e][r] + s:loff[e][r] + s + w], T.zs[:, zoff[e][r] + s:zoff[e][r] + s + w],
+                     T.sem["arr%d" % e], T.sem.sent, pid, rid, topo.mask(core, dst))
+    return 8 * len(plist)
+
+
+def rank_program(g, core, T, topo):
+    route = T.tables["ROUTE"]
+    K = T.tables["K"]
+    n = len(route)
+    me = T.rank_of(core)
+    if me is None:
+        boss = core - HELPER + 7
+        e = T.rank_of(boss) if core % 8 == HELPER else None
+        if e is None:
+            return
+    else:
+        e = me
+    wcols, cnt, zoff, loff, pieces = _plan(route, K)
+
+    spans = []
+    for (r, s, w) in sorted(pieces[e][1], key=lambda p: zoff[e][p[0]] + p[1]):
+        a = zoff[e][r] + s
+        if spans and spans[-1][1] == a:
+            spans[-1][1] = a + w
+        else:
+            spans.append([a, a + w])
+
+    if me is None:
+        g.wait_ge(T.sem.relay, 16 * len(spans))
+        left = _send(g, T, topo, core, e, pieces[e][1], zoff, loff)
+        g.wait_ge(T.sem.sent, left)
+        return
+
+    used = sum(cnt[me])
+    g.sync.dma_start(T.zs[:, 0:used], T.z[:, 0:used]).then_inc(T.sem.zl, 16)
     g.scalar.dma_start(T.gs[:], T.g[:]).then_inc(T.sem.gl, 16)
 
     g.wait_ge(T.sem.zl, 16)
-    order = [(me + d) % n for d in range(1, n)]
-    for r in order:
-        dst = T.cores[r]
-        rid, pid, _se = topo.addr(dst)
-        g.remote_dma(T.land[:, loff[me][r]:loff[me][r] + cnt[me][r]],
-                     T.zs[:, zoff[me][r]:zoff[me][r] + cnt[me][r]],
-                     T.sem["arr%d" % me], T.sem.sent, pid, rid, topo.mask(core, dst))
+    helper = core - 7 + HELPER
+    rid, pid, _se = topo.addr(helper)
+    for (a, b) in spans:
+        g.remote_dma(T.zs[:, a:b], T.zs[:, a:b], T.sem.relay, T.sem.sent, pid, rid, topo.mask(core, helper))
+    left = 16 * len(spans) + _send(g, T, topo, core, me, pieces[me][0], zoff, loff)
 
+    writes = [0] * n
+    late = [0] * n
+    for x in range(n):
+        for via in (0, 1):
+            for (r, s, w) in pieces[x][via]:
+                if r == me:
+                    writes[x] += 1
+                    late[x] = max(late[x], via)
     v = g.vector
     v.wait_ge(T.sem.gl, 16)
     v.wait_ge(T.sem.zl, 16)
     nops = 0
-    for e in [me] + [(me - d) % n for d in range(1, n)]:
-        if e == me:
+    for x in [me] + sorted([x for x in range(n) if x != me], key=lambda x: (late[x], (me - x) % n)):
+        if x == me:
             buf, base = T.zs, zoff[me][me]
         else:
-            buf, base = T.land, loff[e][me]
-            v.wait_ge(T.sem["arr%d" % e], 8)
-        cols = wcols[e][me]
+            buf, base = T.land, loff[x][me]
+            v.wait_ge(T.sem["arr%d" % x], 8 * writes[x])
+        cols = wcols[x][me]
         for (i, m, d) in _runs(cols):
             a = cols[i]
             b = a + (m - 1) * d + 1
@@ -75,4 +141,4 @@ def rank_program(g, core, T, topo):
     g.sync.wait_ge(T.sem.added, 1)
     g.sync.dma_start(T.y[:], T.ys[:]).then_inc(T.sem.stored, 16)
     g.sync.wait_ge(T.sem.stored, 16)
-    g.wait_ge(T.sem.sent, 8 * (n - 1))
+    g.wait_ge(T.sem.sent, left)

from concourse.mybir import AluOpType

NR = 10
HELPER = 3
SCRATCH = {
    "zs": ("sbuf", [128, 1088], "float32"),
    "gs": ("sbuf", [128, 1024], "float32"),
    "land": ("sbuf", [128, 1024], "float32"),
    "prod": ("sbuf", [128, 1024], "float32"),
    "ys": ("sbuf", [128, 512], "float32"),
}
SEMAPHORES = ["zl", "gl", "relay", "sent", "vdone", "added", "stored"] + ["arr%d" % e for e in range(NR)]


def _runs(cols):
    n = len(cols)
    best = [0] + [n + 1] * n
    prev = [0] * (n + 1)
    for i in range(n):
        j = i + 1
        while True:
            if best[i] + 1 < best[j]:
                best[j] = best[i] + 1
                prev[j] = i
            if j >= n or (j - i >= 2 and cols[j] - cols[j - 1] != cols[i + 1] - cols[i]):
                break
            j += 1
    out = []
    j = n
    while j > 0:
        i = prev[j]
        out.append((i, j - i, cols[i + 1] - cols[i] if j - i > 1 else 1))
        j = i
    return out[::-1]


def _plan(route, K):
    n = len(route)
    wcols = [[[t * K + k for t in range(len(route[r])) for k in range(K) if route[r][t][k] == e]
              for r in range(n)] for e in range(n)]
    cnt = [[len(wcols[e][r]) for r in range(n)] for e in range(n)]
    zoff = [[sum(cnt[e][:r]) for r in range(n)] for e in range(n)]
    loff = [[sum(cnt[x][r] for x in range(e)) for r in range(n)] for e in range(n)]
    pieces = []
    for e in range(n):
        m = e ^ 1
        far = [2, 3, 4, 5] if e % 2 == 0 else [5, 6, 7, 8]
        near = [6, 7, 8, 9] if e % 2 == 0 else [1, 2, 3, 4]
        x1 = sum(cnt[e][(e + o) % n] for o in far if o % 2)
        x0 = sum(cnt[e][(e + o) % n] for o in near if o % 2)
        h1 = (cnt[e][m] + x0 - x1) // 2
        h0 = cnt[e][m] - h1
        p0 = [((e + o) % n, 0, cnt[e][(e + o) % n]) for o in near]
        p1 = [((e + o) % n, 0, cnt[e][(e + o) % n]) for o in far]
        if e % 2 == 0:
            p0 = p0 + [(m, 0, h0)]
            p1 = [(m, h0, h1)] + p1
        else:
            p1 = p1 + [(m, 0, h1)]
            p0 = [(m, h1, h0)] + p0
        pieces.append((p0, p1))
    return wcols, cnt, zoff, loff, pieces


def _send(g, T, topo, core, e, plist, zoff, loff):
    for (r, s, w) in plist:
        dst = T.cores[r]
        rid, pid, _se = topo.addr(dst)
        g.remote_dma(T.land[:, loff[e][r] + s:loff[e][r] + s + w], T.zs[:, zoff[e][r] + s:zoff[e][r] + s + w],
                     T.sem["arr%d" % e], T.sem.sent, pid, rid, topo.mask(core, dst))
    return 8 * len(plist)


def rank_program(g, core, T, topo):
    route = T.tables["ROUTE"]
    K = T.tables["K"]
    n = len(route)
    me = T.rank_of(core)
    if me is None:
        boss = core - HELPER + 7
        e = T.rank_of(boss) if core % 8 == HELPER else None
        if e is None:
            return
    else:
        e = me
    wcols, cnt, zoff, loff, pieces = _plan(route, K)

    spans = []
    for (r, s, w) in sorted(pieces[e][1], key=lambda p: zoff[e][p[0]] + p[1]):
        a = zoff[e][r] + s
        if spans and spans[-1][1] == a:
            spans[-1][1] = a + w
        else:
            spans.append([a, a + w])

    if me is None:
        g.wait_ge(T.sem.relay, 16 * len(spans))
        left = _send(g, T, topo, core, e, pieces[e][1], zoff, loff)
        g.wait_ge(T.sem.sent, left)
        return

    used = sum(cnt[me])
    g.sync.dma_start(T.zs[:, 0:used], T.z[:, 0:used]).then_inc(T.sem.zl, 16)
    g.scalar.dma_start(T.gs[:], T.g[:]).then_inc(T.sem.gl, 16)

    g.wait_ge(T.sem.zl, 16)
    helper = core - 7 + HELPER
    rid, pid, _se = topo.addr(helper)
    for (a, b) in spans:
        g.remote_dma(T.zs[:, a:b], T.zs[:, a:b], T.sem.relay, T.sem.sent, pid, rid, topo.mask(core, helper))
    left = 16 * len(spans) + _send(g, T, topo, core, me, pieces[me][0], zoff, loff)

    writes = [0] * n
    late = [0] * n
    for x in range(n):
        for via in (0, 1):
            for (r, s, w) in pieces[x][via]:
                if r == me:
                    writes[x] += 1
                    late[x] = max(late[x], via)
    v = g.vector
    v.wait_ge(T.sem.gl, 16)
    v.wait_ge(T.sem.zl, 16)
    nops = 0
    for x in [me] + sorted([x for x in range(n) if x != me], key=lambda x: (late[x], (me - x) % n)):
        if x == me:
            buf, base = T.zs, zoff[me][me]
        else:
            buf, base = T.land, loff[x][me]
            v.wait_ge(T.sem["arr%d" % x], 8 * writes[x])
        cols = wcols[x][me]
        for (i, m, d) in _runs(cols):
            a = cols[i]
            b = a + (m - 1) * d + 1
            v.tensor_tensor(T.prod[:, a:b:d], T.gs[:, a:b:d], buf[:, base + i:base + i + m],
                            AluOpType.mult).then_inc(T.sem.vdone, 1)
            nops += 1
    v.wait_ge(T.sem.vdone, nops)
    v.tensor_tensor(T.ys[:], T.prod[:, 0::2], T.prod[:, 1::2], AluOpType.add).then_inc(T.sem.added, 1)

    g.sync.wait_ge(T.sem.added, 1)
    g.sync.dma_start(T.y[:], T.ys[:]).then_inc(T.sem.stored, 16)
    g.sync.wait_ge(T.sem.stored, 16)
    g.wait_ge(T.sem.sent, left)
